import numpy as np
import ml_dtypes


def mxq(x, axis, fmt="e4m3"):
    dtype, down = {"e4m3": (ml_dtypes.float8_e4m3fn, 7), "e5m2": (ml_dtypes.float8_e5m2, 14)}[fmt]
    v = np.moveaxis(np.asarray(x, np.float32).astype(ml_dtypes.bfloat16).astype(np.float64), axis, -1)
    blocks = v.reshape(v.shape[:-1] + (-1, 32))
    amax = np.abs(blocks).max(-1, keepdims=True)
    byte = np.maximum(np.where(amax > 0, np.frexp(amax)[1] - 1 + 127, 0) - down, 1)
    scale = np.exp2(byte - 127.0)
    codes = (blocks / scale).astype(np.float32).astype(dtype).astype(np.float64)
    return np.moveaxis((codes * scale).reshape(v.shape), -1, axis)


WIDE = False


def mx_kscale(k):
    if not WIDE:
        return np.ones(k)
    levels = np.array([10, -10, 5, -5, 0])
    if k % 512:
        return np.exp2(np.random.permutation(np.resize(levels, k // 32))).repeat(32)
    a = np.empty((k // 512, 16))
    for p in range(k // 512):
        a[p, :8] = np.random.permutation(np.resize(levels, 8))
        for g in range(8):
            far = levels[np.abs(levels - a[p, g]) >= 10]
            a[p, g + 8] = far[np.random.randint(len(far))]
    return np.exp2(a.ravel()).repeat(32)


def f64(x):
    return np.asarray(x).astype(np.float64)


def striped(idx):
    return np.tile(idx.reshape(-1, 16).T, (8, 1)).astype(np.uint16)


def unstriped(offs):
    return offs[:16].T.reshape(-1).astype(np.int64)


def pack_weight(w):
    k, n = w.shape
    w = f64(np.asarray(w, np.float32).astype(ml_dtypes.bfloat16)).reshape(k // 32, 32, n)
    amax = np.abs(w).max(1)
    byte = np.clip(np.where(amax > 0, np.frexp(amax)[1] - 1 + 127 - 7, 1), 1, 254)
    scaled = (w * np.exp2(127.0 - byte)[:, None, :]).reshape(k, n).astype(np.float32)
    words = np.ascontiguousarray(scaled.reshape(k // 512, 128, 4, n).transpose(0, 1, 3, 2)).astype(ml_dtypes.float8_e4m3fn).view(np.uint8)
    return words, np.ascontiguousarray(byte.astype(np.uint8).reshape(k // 512, 16, n))


def unpack_weight(words, scales):
    g, p, n, _ = words.shape
    vals = np.ascontiguousarray(words).view(ml_dtypes.float8_e4m3fn).astype(np.float64) * np.repeat(np.exp2(scales.astype(np.float64) - 127.0), 8, axis=1)[..., None]
    return vals.transpose(0, 1, 3, 2).reshape(g * 512, n)


def sigmoid(v):
    return 1.0 / (1.0 + np.exp(-np.maximum(v, -700.0)))


K, T, S, D, N, H = 512, 1024, 512, 4, 128, 512


def setup_inputs():
    n = np.random.standard_normal
    s = mx_kscale(K)[:, None]
    u = mx_kscale(H)
    packed_xT = pack_weight(n((K, T)) * s)
    return {
        "x_words": packed_xT[0],
        "x_scales": packed_xT[1],
        "w1": (n((K, H)) / np.sqrt(K) / s).astype(np.float32),
        "w2": (n((K, H)) / np.sqrt(K) / s).astype(np.float32),
        "ff": (np.random.uniform(0.05, 0.4, (H, S))).astype(np.float32),
        "unit": (np.random.uniform(0.6, 1.4, (H, 1)) * u[:, None]).astype(np.float32),
        "w3": (n((H, N)) / np.sqrt(H) / u[:, None]).astype(np.float32),
        "offs": striped(np.random.permutation(T)[:S]),
        "see": striped(np.random.permutation(S)),
    }


def reference(x_words, x_scales, w1, w2, ff, unit, w3, offs, see):
    xq = unpack_weight(x_words, x_scales)[:, unstriped(offs)]
    em = mxq(f64(w1), 0, "e4m3").T @ xq
    emi = np.log(np.exp(em) + 1.0)
    rf = mxq(f64(w2), 0, "e4m3").T @ xq
    rho = 0.9 * sigmoid(rf)
    es = emi[:, unstriped(see)]
    ef = es * f64(ff)
    inc = ef.reshape(len(ef), -1, D).sum(axis=2)
    bone = emi + rho * np.repeat(inc, D, axis=1)
    bs = bone[:, unstriped(see)]
    bf = bs * f64(ff)
    inc2 = bf.reshape(len(bf), -1, D).sum(axis=2)
    hid = f64(unit) * (emi + rho * np.repeat(inc2, D, axis=1))
    return mxq(f64(w3), 0, "e4m3").T @ mxq(hid, 0, "e4m3")

@@ -1,0 +1,204 @@
+from contextlib import ExitStack
+
+import concourse.mybir as mybir
+from concourse.masks import make_identity
+
+K, T, S, D, N, H = 512, 1024, 512, 4, 128, 512
+FLOPS = 2 * K * H * S * 2 + 2 * H * N * S
+
+F32 = mybir.dt.float32
+BF16 = mybir.dt.bfloat16
+I32 = mybir.dt.int32
+U32 = mybir.dt.uint32
+U16 = mybir.dt.uint16
+U8 = mybir.dt.uint8
+FP8X4 = mybir.dt.float8_e4m3fn_x4
+ACT = mybir.ActivationFunctionType
+ALU = mybir.AluOpType
+
+P = 128
+PACK = 4
+V = S // D
+LN_FLOOR = 2.0 ** -60
+FUSED1 = (0, 1, 2, 3)
+FUSED2 = ()
+COPY_V = ((0, 0), (0, 1))
+MULT_G = ()
+ORDER = "R0 R1 R2 R3 A0 A1 A2 A3 B0 B1 B2 B3 C0 C1 C2 C3"
+
+
+def tile_picked_yradio_two_p_kernel(tc, x_words, x_scales, w1, w2, ff, unit, w3, offs, see, out):
+    nc = tc.nc
+    with ExitStack() as ctx:
+        keep = ctx.enter_context(tc.tile_pool(name="keep", bufs=1))
+        psum = ctx.enter_context(tc.psum_pool(name="psum", bufs=1))
+
+        offs_sb = keep.tile([P, S // 16], U16, name="offs_sb")
+        see_sb = keep.tile([P, S // 16], U16, name="see_sb")
+        xs_all = keep.tile([P, T], U8, name="xs_all", align_bytes=64)
+        xw_all = keep.tile([P, T], U32, name="xw_all", align_bytes=64)
+        nc.vector.memset(xs_all[:].bitcast(I32), 0)
+        nc.sync.dma_start(offs_sb[:], offs)
+        for q in range(4):
+            nc.sync.dma_start(xs_all[32 * q : 32 * q + 4, :].bitcast(I32), x_scales[0, 4 * q : 4 * q + 4, :].bitcast(I32))
+        nc.sync.dma_start(xw_all[:].bitcast(I32), x_words[0].rearrange("p n r -> p (n r)").bitcast(I32))
+        w1_raw = [keep.tile([P, PACK, H // 2], F32, name=f"w1_raw{h}") for h in range(2)]
+        for h in range(2):
+            nc.sync.dma_start(w1_raw[h][:], w1.rearrange("(p j) c -> p j c", j=PACK)[:, :, h * (H // 2) : (h + 1) * (H // 2)])
+        w2_raw = keep.tile([P, PACK, H], F32, name="w2_raw")
+        nc.sync.dma_start(w2_raw[:], w2.rearrange("(p j) c -> p j c", j=PACK))
+        nc.sync.dma_start(see_sb[:], see)
+        ff_sb = [keep.tile([P, 2, S], F32, name=f"ff_sb{h}") for h in range(2)]
+        for h in range(2):
+            nc.sync.dma_start(ff_sb[h][:], ff.rearrange("(p t) c -> p t c", t=PACK)[:, 2 * h : 2 * h + 2, :])
+        w3_raw = keep.tile([P, PACK, N], F32, name="w3_raw")
+        nc.sync.dma_start(w3_raw[:], w3.rearrange("(p j) c -> p j c", j=PACK))
+        unit_sb = keep.tile([P, PACK], F32, name="unit_sb")
+        nc.sync.dma_start(unit_sb[:], unit.rearrange("(p t) o -> p (t o)", t=PACK))
+
+        ident = keep.tile([P, P], F32, name="ident")
+        make_identity(nc, ident[:])
+        floor = keep.tile([P, 1], F32, name="floor")
+        nc.gpsimd.memset(floor[:], LN_FLOOR)
+
+        xw = keep.tile([P, S], U32, name="xw", align_bytes=64)
+        xs = keep.tile([P, S], U8, name="xs", align_bytes=64)
+        nc.vector.tensor_copy(xs[:], xs_all[:].indirect(offs_sb[:]))
+        nc.vector.tensor_copy(xw[:], xw_all[:].indirect(offs_sb[:]))
+
+        def dealt_cast(grouped, raw, m0, m1):
+            nc.vector.tensor_copy(
+                out=grouped[:, :, m0:m1, :].rearrange("p t m j -> p m j t"),
+                in_=raw[:].rearrange("p j (m t) -> p m j t", t=PACK),
+            )
+
+        def product(bank, codes, scales, t):
+            nc.tensor.matmul_mx(
+                out=bank[:], lhsT=codes[:, t, :].bitcast(FP8X4), lhsT_scale=scales[:, t, :],
+                rhs=xw[:].bitcast(FP8X4), rhs_scale=xs[:], start=True, stop=True,
+            )
+
+        em = [psum.tile([P, S], F32, name=f"em{t}") for t in range(PACK)]
+        rf = [psum.tile([P, S], F32, name=f"rf{t}") for t in range(PACK)]
+
+        w1_bf = keep.tile([P, PACK, P, PACK], BF16, name="w1_bf", align_bytes=64)
+        w1_codes = keep.tile([P, PACK, P], U32, name="w1_codes", align_bytes=64)
+        w1_scales = keep.tile([P, PACK, P], U8, name="w1_scales", align_bytes=64)
+        for h in range(2):
+            dealt_cast(w1_bf, w1_raw[h], h * (P // 2), (h + 1) * (P // 2))
+        sig_em = keep.tile([P, PACK, S], F32, name="sig_em")
+        for t in range(PACK):
+            nc.vector.quantize_mx(out=w1_codes[:, t, :].bitcast(FP8X4), scales=w1_scales[:, t, :], in_=w1_bf[:, t, :, :].rearrange("p m j -> p (m j)"))
+            product(em[t], w1_codes, w1_scales, t)
+            nc.scalar.activation(sig_em[:, t, :], em[t][:], ACT.Sigmoid, scale=-1.0)
+
+        w2_bf = keep.tile([P, PACK, P, PACK], BF16, name="w2_bf", align_bytes=64)
+        w2_codes = keep.tile([P, PACK, P], U32, name="w2_codes", align_bytes=64)
+        w2_scales = keep.tile([P, PACK, P], U8, name="w2_scales", align_bytes=64)
+        dealt_cast(w2_bf, w2_raw, 0, P)
+        nc.vector.quantize_mx(
+            out=w2_codes[:].rearrange("p t m -> p (t m)").bitcast(FP8X4),
+            scales=w2_scales[:].rearrange("p t m -> p (t m)"),
+            in_=w2_bf[:].rearrange("p t m j -> p (t m j)"),
+        )
+        for t in range(PACK):
+            product(rf[t], w2_codes, w2_scales, t)
+
+        w3_bf = keep.tile([P, N, PACK], BF16, name="w3_bf", align_bytes=64)
+        w3_codes = keep.tile([P, N], U32, name="w3_codes", align_bytes=64)
+        w3_scales = keep.tile([P, N], U8, name="w3_scales", align_bytes=64)
+        unit9 = keep.tile([P, PACK], F32, name="unit9")
+
+        emi_win = [keep.tile([P, 2 * S], F32, name=f"emi_win{t}") for t in range(PACK)]
+        for t in range(PACK):
+            nc.scalar.activation(emi_win[t][:, S:], sig_em[:, t, :], ACT.Ln, bias=floor[:])
+        nc.vector.tensor_copy(
+            out=w3_bf[:].rearrange("p (c i) j -> p c j i", i=4),
+            in_=w3_raw[:].rearrange("p j (c i) -> p c j i", i=4),
+        )
+        nc.vector.tensor_scalar(unit9[:], unit_sb[:], 0.9, None, ALU.mult)
+        nc.vector.quantize_mx(out=w3_codes[:].bitcast(FP8X4), scales=w3_scales[:], in_=w3_bf[:].rearrange("p m j -> p (m j)"))
+
+        sig_rf = keep.tile([P, PACK, S], F32, name="sig_rf")
+        refl_win = [keep.tile([P, S + V], F32, name=f"refl_win{t}") for t in range(PACK)]
+        sent = [[keep.tile([P, S], F32, name=f"sent{b}_{t}") for t in range(PACK)] for b in range(2)]
+        picked = [[keep.tile([P, S], F32, name=f"picked{b}_{t}") for t in range(PACK)] for b in range(2)]
+        more_t = [keep.tile([P, V], F32, name=f"more_t{t}") for t in range(PACK)]
+        refl2 = [keep.tile([P, S], F32, name=f"refl2_{t}") for t in range(PACK)]
+        hid_rows = keep.tile([P, PACK, S], BF16, name="hid_rows")
+
+        def gather_times_ff(b, t, window, fused):
+            form = ff_sb[t // 2][:, t % 2, :]
+            if fused:
+                nc.vector.tensor_tensor(sent[b][t][:], window[:].indirect(see_sb[:]), form, ALU.mult)
+            else:
+                nc.scalar.activation(picked[b][t][:], window[:].indirect(see_sb[:]), ACT.Copy)
+                if (b, t) in MULT_G:
+                    nc.gpsimd.tensor_tensor(sent[b][t][:], picked[b][t][:], form, ALU.mult)
+                else:
+                    nc.vector.tensor_tensor(sent[b][t][:], picked[b][t][:], form, ALU.mult)
+
+        def group_sums(b, t, dst, parts):
+            bank = em[t]
+            for d in range(D):
+                nc.tensor.matmul(bank[:, 0:P], lhsT=sent[b][t][:, d:S:D], rhs=ident[:], is_transpose=True, start=(d == 0), stop=(d == D - 1))
+            if (b, t) in COPY_V:
+                nc.vector.tensor_copy(dst, bank[:, 0:P])
+            else:
+                nc.scalar.copy(dst, bank[:, 0:P])
+            for n, part in enumerate(parts):
+                nc.tensor.matmul(bank[:, P : 2 * P], lhsT=part, rhs=ident[:], is_transpose=True, start=(n == 0), stop=(n == len(parts) - 1))
+
+        def sums_by_member(t, v0, v1):
+            return em[t][:, P + v0 : P + v1].unsqueeze(2).to_broadcast([P, v1 - v0, D])
+
+        def reflectance(t):
+            nc.scalar.activation(sig_rf[:, t, :], rf[t][:], ACT.Sigmoid)
+
+        def first_bounce(t):
+            nc.vector.scalar_tensor_tensor(emi_win[t][:, 0:S], emi_win[t][:, S:], -1.0, em[t][:], ALU.mult, ALU.max)
+            gather_times_ff(0, t, emi_win[t], t in FUSED1)
+            group_sums(0, t, refl_win[t][:, S:], [refl_win[t][:, S:]])
+
+        def second_bounce(t):
+            nc.vector.scalar_tensor_tensor(
+                refl_win[t][:, 0:S].rearrange("p (v d) -> p v d", d=D),
+                sig_rf[:, t, :].rearrange("p (v d) -> p v d", d=D), 0.9, sums_by_member(t, 0, V), ALU.mult, ALU.mult,
+            )
+            gather_times_ff(1, t, refl_win[t], t in FUSED2)
+            group_sums(1, t, more_t[t][:], [refl_win[t][:, S:], more_t[t][:]])
+
+        def hidden(t):
+            pieces = 2 if t == PACK - 1 else 1
+            for n in range(pieces):
+                v0, v1 = n * V // pieces, (n + 1) * V // pieces
+                cols = slice(D * v0, D * v1)
+                nc.vector.scalar_tensor_tensor(
+                    refl2[t][:, cols].rearrange("p (v d) -> p v d", d=D),
+                    sig_rf[:, t, cols].rearrange("p (v d) -> p v d", d=D), unit9[:, t : t + 1], sums_by_member(t, v0, v1), ALU.mult, ALU.mult,
+                )
+                nc.vector.scalar_tensor_tensor(hid_rows[:, t, cols], emi_win[t][:, cols], unit_sb[:, t : t + 1], refl2[t][:, cols], ALU.mult, ALU.add)
+
+        steps = {"R": reflectance, "A": first_bounce, "B": second_bounce, "C": hidden}
+        for step in ORDER.split():
+            steps[step[0]](int(step[1]))
+
+        half = S // 2
+        for h in range(2):
+            hid_bf = keep.tile([P, half, PACK], BF16, name=f"hid_bf{h}", align_bytes=64)
+            hid_codes = keep.tile([P, half], U32, name=f"hid_codes{h}", align_bytes=64)
+            hid_scales = keep.tile([P, half], U8, name=f"hid_scales{h}", align_bytes=64)
+            res = keep.tile([P, half], F32, name=f"res{h}")
+            dst = hid_bf[:].rearrange("p (c i) t -> p c t i", i=4)
+            src = hid_rows[:, :, h * half : (h + 1) * half].rearrange("p t (c i) -> p c t i", i=4)
+            nc.vector.tensor_copy(out=dst, in_=src)
+            nc.vector.quantize_mx(out=hid_codes[:].bitcast(FP8X4), scales=hid_scales[:], in_=hid_bf[:].rearrange("p c t -> p (c t)"))
+            nc.tensor.matmul_mx(
+                out=rf[h][:, 0:half], lhsT=w3_codes[:].bitcast(FP8X4), lhsT_scale=w3_scales[:],
+                rhs=hid_codes[:].bitcast(FP8X4), rhs_scale=hid_scales[:], start=True, stop=True,
+            )
+            if h == 0:
+                nc.scalar.copy(res[:], rf[h][:, 0:half])
+            else:
+                nc.vector.tensor_copy(res[:], rf[h][:, 0:half])
+            nc.sync.dma_start(out[:, h * half : (h + 1) * half], res[:])

@@ -18,13 +18,12 @@ ALU = mybir.AluOpType
 
 P = 128
 PACK = 4
-V = S // D
-LN_FLOOR = 2.0 ** -60
-FUSED1 = (0, 1, 2, 3)
-FUSED2 = ()
-COPY_V = ((0, 0), (0, 1))
-MULT_G = ()
-ORDER = "R0 R1 R2 R3 A0 A1 A2 A3 B0 B1 B2 B3 C0 C1 C2 C3"
+LIST_ROWS = 16
+HALF = S // 2
+GROUPS = 2 * HALF // D
+RUN = 4
+LN_FLOOR = 2.0**-60
+OUT_PIECES = ((0, 256), (256, 384), (384, 512))
 
 
 def tile_picked_yradio_two_p_kernel(tc, x_words, x_scales, w1, w2, ff, unit, w3, offs, see, out):
@@ -33,49 +32,64 @@ def tile_picked_yradio_two_p_kernel(tc, x_words, x_scales, w1, w2, ff, unit, w3,
         keep = ctx.enter_context(tc.tile_pool(name="keep", bufs=1))
         psum = ctx.enter_context(tc.psum_pool(name="psum", bufs=1))
 
-        offs_sb = keep.tile([P, S // 16], U16, name="offs_sb")
-        see_sb = keep.tile([P, S // 16], U16, name="see_sb")
-        xs_all = keep.tile([P, T], U8, name="xs_all", align_bytes=64)
-        xw_all = keep.tile([P, T], U32, name="xw_all", align_bytes=64)
-        nc.vector.memset(xs_all[:].bitcast(I32), 0)
-        nc.sync.dma_start(offs_sb[:], offs)
-        for q in range(4):
-            nc.sync.dma_start(xs_all[32 * q : 32 * q + 4, :].bitcast(I32), x_scales[0, 4 * q : 4 * q + 4, :].bitcast(I32))
-        nc.sync.dma_start(xw_all[:].bitcast(I32), x_words[0].rearrange("p n r -> p (n r)").bitcast(I32))
-        w1_raw = [keep.tile([P, PACK, H // 2], F32, name=f"w1_raw{h}") for h in range(2)]
-        for h in range(2):
-            nc.sync.dma_start(w1_raw[h][:], w1.rearrange("(p j) c -> p j c", j=PACK)[:, :, h * (H // 2) : (h + 1) * (H // 2)])
+        offs_sb = keep.tile([P, S // LIST_ROWS], U16, name="offs_sb")
+        see_sb = keep.tile([P, S // LIST_ROWS], U16, name="see_sb")
+        table_scales = keep.tile([P, T], U8, name="table_scales", align_bytes=64)
+        table_words = keep.tile([P, T], U32, name="table_words", align_bytes=64)
+        w1_raw = keep.tile([P, PACK, H], F32, name="w1_raw")
         w2_raw = keep.tile([P, PACK, H], F32, name="w2_raw")
+        w3_raw = keep.tile([P, PACK, N], F32, name="w3_raw")
+        unit_sb = keep.tile([P, PACK], F32, name="unit_sb")
+        ff_sb = [keep.tile([P, 2, S], F32, name=f"ff_sb{pair}") for pair in range(2)]
+
+        nc.gpsimd.memset(table_scales[:].bitcast(I32), 0)
+        nc.sync.dma_start(offs_sb[:], offs)
+        for quad in range(4):
+            nc.sync.dma_start(
+                table_scales[32 * quad : 32 * quad + 4, :].bitcast(I32),
+                x_scales[0, 4 * quad : 4 * quad + 4, :].bitcast(I32),
+            )
+        nc.sync.dma_start(table_words[:].bitcast(I32), x_words[0].rearrange("p c r -> p (c r)").bitcast(I32))
+        nc.sync.dma_start(w1_raw[:], w1.rearrange("(p j) c -> p j c", j=PACK))
         nc.sync.dma_start(w2_raw[:], w2.rearrange("(p j) c -> p j c", j=PACK))
         nc.sync.dma_start(see_sb[:], see)
-        ff_sb = [keep.tile([P, 2, S], F32, name=f"ff_sb{h}") for h in range(2)]
-        for h in range(2):
-            nc.sync.dma_start(ff_sb[h][:], ff.rearrange("(p t) c -> p t c", t=PACK)[:, 2 * h : 2 * h + 2, :])
-        w3_raw = keep.tile([P, PACK, N], F32, name="w3_raw")
-        nc.sync.dma_start(w3_raw[:], w3.rearrange("(p j) c -> p j c", j=PACK))
-        unit_sb = keep.tile([P, PACK], F32, name="unit_sb")
         nc.sync.dma_start(unit_sb[:], unit.rearrange("(p t) o -> p (t o)", t=PACK))
+        for pair in range(2):
+            nc.sync.dma_start(ff_sb[pair][:], ff.rearrange("(p t) c -> p t c", t=PACK)[:, 2 * pair : 2 * pair + 2, :])
+        nc.sync.dma_start(w3_raw[:], w3.rearrange("(p j) c -> p j c", j=PACK))
 
         ident = keep.tile([P, P], F32, name="ident")
         make_identity(nc, ident[:])
-        floor = keep.tile([P, 1], F32, name="floor")
-        nc.gpsimd.memset(floor[:], LN_FLOOR)
+        ln_floor = keep.tile([P, 1], F32, name="ln_floor")
+        nc.gpsimd.memset(ln_floor[:], LN_FLOOR)
 
-        xw = keep.tile([P, S], U32, name="xw", align_bytes=64)
-        xs = keep.tile([P, S], U8, name="xs", align_bytes=64)
-        nc.vector.tensor_copy(xs[:], xs_all[:].indirect(offs_sb[:]))
-        nc.vector.tensor_copy(xw[:], xw_all[:].indirect(offs_sb[:]))
+        x_codes = keep.tile([P, S], U32, name="x_codes", align_bytes=64)
+        x_planes = keep.tile([P, S], U8, name="x_planes", align_bytes=64)
+        nc.vector.tensor_copy(x_planes[:], table_scales[:].indirect(offs_sb[:]))
+        nc.vector.tensor_copy(x_codes[:], table_words[:].indirect(offs_sb[:]))
 
-        def dealt_cast(grouped, raw, m0, m1):
+        def deal_and_round(rounded, raw, t0, t1):
             nc.vector.tensor_copy(
-                out=grouped[:, :, m0:m1, :].rearrange("p t m j -> p m j t"),
-                in_=raw[:].rearrange("p j (m t) -> p m j t", t=PACK),
+                out=rounded[:, t0:t1, :, :].rearrange("p t m j -> p m j t"),
+                in_=raw[:].rearrange("p j (m t) -> p m j t", t=PACK)[:, :, :, t0:t1],
             )
 
-        def product(bank, codes, scales, t):
+        def quantise(codes, scales, rounded, t0, t1):
+            nc.vector.quantize_mx(
+                out=codes[:, t0:t1, :].rearrange("p t m -> p (t m)").bitcast(FP8X4),
+                scales=scales[:, t0:t1, :].rearrange("p t m -> p (t m)"),
+                in_=rounded[:, t0:t1, :, :].rearrange("p t m j -> p (t m j)"),
+            )
+
+        def times_patches(bank, codes, scales, t):
             nc.tensor.matmul_mx(
-                out=bank[:], lhsT=codes[:, t, :].bitcast(FP8X4), lhsT_scale=scales[:, t, :],
-                rhs=xw[:].bitcast(FP8X4), rhs_scale=xs[:], start=True, stop=True,
+                out=bank[:],
+                lhsT=codes[:, t, :].bitcast(FP8X4),
+                lhsT_scale=scales[:, t, :],
+                rhs=x_codes[:].bitcast(FP8X4),
+                rhs_scale=x_planes[:],
+                start=True,
+                stop=True,
             )
 
         em = [psum.tile([P, S], F32, name=f"em{t}") for t in range(PACK)]
@@ -84,121 +98,182 @@ def tile_picked_yradio_two_p_kernel(tc, x_words, x_scales, w1, w2, ff, unit, w3,
         w1_bf = keep.tile([P, PACK, P, PACK], BF16, name="w1_bf", align_bytes=64)
         w1_codes = keep.tile([P, PACK, P], U32, name="w1_codes", align_bytes=64)
         w1_scales = keep.tile([P, PACK, P], U8, name="w1_scales", align_bytes=64)
-        for h in range(2):
-            dealt_cast(w1_bf, w1_raw[h], h * (P // 2), (h + 1) * (P // 2))
-        sig_em = keep.tile([P, PACK, S], F32, name="sig_em")
-        for t in range(PACK):
-            nc.vector.quantize_mx(out=w1_codes[:, t, :].bitcast(FP8X4), scales=w1_scales[:, t, :], in_=w1_bf[:, t, :, :].rearrange("p m j -> p (m j)"))
-            product(em[t], w1_codes, w1_scales, t)
-            nc.scalar.activation(sig_em[:, t, :], em[t][:], ACT.Sigmoid, scale=-1.0)
+        sig_neg_em = keep.tile([P, PACK, S], F32, name="sig_neg_em")
+        for pair in range(2):
+            deal_and_round(w1_bf, w1_raw, 2 * pair, 2 * pair + 2)
+            for t in (2 * pair, 2 * pair + 1):
+                quantise(w1_codes, w1_scales, w1_bf, t, t + 1)
+                times_patches(em[t], w1_codes, w1_scales, t)
+                nc.scalar.activation(sig_neg_em[:, t, :], em[t][:], ACT.Sigmoid, scale=-1.0)
 
         w2_bf = keep.tile([P, PACK, P, PACK], BF16, name="w2_bf", align_bytes=64)
         w2_codes = keep.tile([P, PACK, P], U32, name="w2_codes", align_bytes=64)
         w2_scales = keep.tile([P, PACK, P], U8, name="w2_scales", align_bytes=64)
-        dealt_cast(w2_bf, w2_raw, 0, P)
-        nc.vector.quantize_mx(
-            out=w2_codes[:].rearrange("p t m -> p (t m)").bitcast(FP8X4),
-            scales=w2_scales[:].rearrange("p t m -> p (t m)"),
-            in_=w2_bf[:].rearrange("p t m j -> p (t m j)"),
-        )
+        deal_and_round(w2_bf, w2_raw, 0, PACK)
+        quantise(w2_codes, w2_scales, w2_bf, 0, PACK)
         for t in range(PACK):
-            product(rf[t], w2_codes, w2_scales, t)
+            times_patches(rf[t], w2_codes, w2_scales, t)
+
+        ff_unit = [keep.tile([P, 2, S], F32, name=f"ff_unit{pair}") for pair in range(2)]
+        for t in range(PACK):
+            nc.vector.tensor_scalar(ff_unit[t // 2][:, t % 2, :], ff_sb[t // 2][:, t % 2, :], unit_sb[:, t : t + 1], None, ALU.mult)
 
         w3_bf = keep.tile([P, N, PACK], BF16, name="w3_bf", align_bytes=64)
         w3_codes = keep.tile([P, N], U32, name="w3_codes", align_bytes=64)
         w3_scales = keep.tile([P, N], U8, name="w3_scales", align_bytes=64)
-        unit9 = keep.tile([P, PACK], F32, name="unit9")
-
-        emi_win = [keep.tile([P, 2 * S], F32, name=f"emi_win{t}") for t in range(PACK)]
-        for t in range(PACK):
-            nc.scalar.activation(emi_win[t][:, S:], sig_em[:, t, :], ACT.Ln, bias=floor[:])
         nc.vector.tensor_copy(
-            out=w3_bf[:].rearrange("p (c i) j -> p c j i", i=4),
-            in_=w3_raw[:].rearrange("p j (c i) -> p c j i", i=4),
+            out=w3_bf[:].rearrange("p (c i) j -> p c j i", i=RUN),
+            in_=w3_raw[:].rearrange("p j (c i) -> p c j i", i=RUN),
         )
-        nc.vector.tensor_scalar(unit9[:], unit_sb[:], 0.9, None, ALU.mult)
         nc.vector.quantize_mx(out=w3_codes[:].bitcast(FP8X4), scales=w3_scales[:], in_=w3_bf[:].rearrange("p m j -> p (m j)"))
 
+        log_sig = keep.tile([P, PACK, S], F32, name="log_sig")
+        for t in range(PACK):
+            nc.scalar.activation(log_sig[:, t, :], sig_neg_em[:, t, :], ACT.Ln, bias=ln_floor[:])
+
+        emi = [keep.tile([P, S], F32, name=f"emi{t}") for t in range(PACK)]
         sig_rf = keep.tile([P, PACK, S], F32, name="sig_rf")
-        refl_win = [keep.tile([P, S + V], F32, name=f"refl_win{t}") for t in range(PACK)]
-        sent = [[keep.tile([P, S], F32, name=f"sent{b}_{t}") for t in range(PACK)] for b in range(2)]
-        picked = [[keep.tile([P, S], F32, name=f"picked{b}_{t}") for t in range(PACK)] for b in range(2)]
-        more_t = [keep.tile([P, V], F32, name=f"more_t{t}") for t in range(PACK)]
-        refl2 = [keep.tile([P, S], F32, name=f"refl2_{t}") for t in range(PACK)]
-        hid_rows = keep.tile([P, PACK, S], BF16, name="hid_rows")
 
-        def gather_times_ff(b, t, window, fused):
-            form = ff_sb[t // 2][:, t % 2, :]
-            if fused:
-                nc.vector.tensor_tensor(sent[b][t][:], window[:].indirect(see_sb[:]), form, ALU.mult)
-            else:
-                nc.scalar.activation(picked[b][t][:], window[:].indirect(see_sb[:]), ACT.Copy)
-                if (b, t) in MULT_G:
-                    nc.gpsimd.tensor_tensor(sent[b][t][:], picked[b][t][:], form, ALU.mult)
-                else:
-                    nc.vector.tensor_tensor(sent[b][t][:], picked[b][t][:], form, ALU.mult)
-
-        def group_sums(b, t, dst, parts):
-            bank = em[t]
-            for d in range(D):
-                nc.tensor.matmul(bank[:, 0:P], lhsT=sent[b][t][:, d:S:D], rhs=ident[:], is_transpose=True, start=(d == 0), stop=(d == D - 1))
-            if (b, t) in COPY_V:
-                nc.vector.tensor_copy(dst, bank[:, 0:P])
-            else:
-                nc.scalar.copy(dst, bank[:, 0:P])
-            for n, part in enumerate(parts):
-                nc.tensor.matmul(bank[:, P : 2 * P], lhsT=part, rhs=ident[:], is_transpose=True, start=(n == 0), stop=(n == len(parts) - 1))
-
-        def sums_by_member(t, v0, v1):
-            return em[t][:, P + v0 : P + v1].unsqueeze(2).to_broadcast([P, v1 - v0, D])
+        def emission(t):
+            nc.vector.scalar_tensor_tensor(emi[t][:], log_sig[:, t, :], -1.0, em[t][:], ALU.mult, ALU.max)
 
         def reflectance(t):
             nc.scalar.activation(sig_rf[:, t, :], rf[t][:], ACT.Sigmoid)
 
-        def first_bounce(t):
-            nc.vector.scalar_tensor_tensor(emi_win[t][:, 0:S], emi_win[t][:, S:], -1.0, em[t][:], ALU.mult, ALU.max)
-            gather_times_ff(0, t, emi_win[t], t in FUSED1)
-            group_sums(0, t, refl_win[t][:, S:], [refl_win[t][:, S:]])
+        def bank_of(pair, half):
+            return em[2 * pair + half]
 
-        def second_bounce(t):
+        def columns(half):
+            return slice(half * HALF, (half + 1) * HALF)
+
+        def entries(half):
+            return see_sb[:, half * (HALF // LIST_ROWS) : (half + 1) * (HALF // LIST_ROWS)]
+
+        def in_groups(rows):
+            return rows.rearrange("p e (v d) -> p e v d", d=D)
+
+        def fetch(picked, windows, half):
+            for e in range(2):
+                nc.scalar.activation(picked[:, e * HALF : (e + 1) * HALF], windows[e].indirect(entries(half)), ACT.Copy)
+
+        def weigh(sent, picked, factors, half):
+            nc.vector.tensor_tensor(sent, picked.rearrange("p (e v d) -> p e v d", e=2, d=D), in_groups(factors[:, :, columns(half)]), ALU.mult)
+
+        def add_turned(target, terms):
+            for n, term in enumerate(terms):
+                nc.tensor.matmul(target, lhsT=term, rhs=ident[:], is_transpose=True, start=(n == 0), stop=(n == len(terms) - 1))
+
+        def reflect(target, pair, half, sums):
+            repeated = sums.rearrange("p (e v) -> p e v", e=2).unsqueeze(3).to_broadcast([P, 2, GROUPS // 2, D])
             nc.vector.scalar_tensor_tensor(
-                refl_win[t][:, 0:S].rearrange("p (v d) -> p v d", d=D),
-                sig_rf[:, t, :].rearrange("p (v d) -> p v d", d=D), 0.9, sums_by_member(t, 0, V), ALU.mult, ALU.mult,
+                in_groups(target[:, :, columns(half)]),
+                in_groups(sig_rf[:, 2 * pair : 2 * pair + 2, columns(half)]),
+                0.9,
+                repeated,
+                ALU.mult,
+                ALU.mult,
             )
-            gather_times_ff(1, t, refl_win[t], t in FUSED2)
-            group_sums(1, t, more_t[t][:], [refl_win[t][:, S:], more_t[t][:]])
 
-        def hidden(t):
-            pieces = 2 if t == PACK - 1 else 1
-            for n in range(pieces):
-                v0, v1 = n * V // pieces, (n + 1) * V // pieces
-                cols = slice(D * v0, D * v1)
-                nc.vector.scalar_tensor_tensor(
-                    refl2[t][:, cols].rearrange("p (v d) -> p v d", d=D),
-                    sig_rf[:, t, cols].rearrange("p (v d) -> p v d", d=D), unit9[:, t : t + 1], sums_by_member(t, v0, v1), ALU.mult, ALU.mult,
+        parts = [(pair, half) for pair in range(2) for half in range(2)]
+        inc = {}
+        inc_turned = {}
+
+        for t in (0, 1):
+            reflectance(t)
+        for t in (0, 1):
+            emission(t)
+        for half in range(2):
+            sent = keep.tile([P, 2 * HALF], F32, name=f"sent_first0{half}")
+            for e in range(2):
+                nc.vector.tensor_tensor(
+                    sent[:, e * HALF : (e + 1) * HALF], emi[e][:].indirect(entries(half)), ff_unit[0][:, e, columns(half)], ALU.mult
                 )
-                nc.vector.scalar_tensor_tensor(hid_rows[:, t, cols], emi_win[t][:, cols], unit_sb[:, t : t + 1], refl2[t][:, cols], ALU.mult, ALU.add)
+            bank = bank_of(0, half)
+            add_turned(bank[:, 0:GROUPS], [sent[:, d : 2 * HALF : D] for d in range(D)])
+            turned = keep.tile([P, GROUPS], F32, name=f"inc_turned{half}")
+            nc.vector.tensor_copy(turned[:], bank[:, 0:GROUPS])
+            add_turned(bank[:, GROUPS : 2 * GROUPS], [turned[:]])
+            inc_turned[0, half] = turned[:]
+            inc[0, half] = bank[:, GROUPS : 2 * GROUPS]
 
-        steps = {"R": reflectance, "A": first_bounce, "B": second_bounce, "C": hidden}
-        for step in ORDER.split():
-            steps[step[0]](int(step[1]))
+        for t in (2, 3):
+            emission(t)
+        for half in range(2):
+            picked = keep.tile([P, 2 * HALF], F32, name=f"picked_first{half}")
+            sent = keep.tile([P, 2 * HALF], F32, name=f"sent_first1{half}")
+            sums = keep.tile([P, GROUPS], F32, name=f"inc_plain{half}")
+            fetch(picked, [emi[2][:], emi[3][:]], half)
+            weigh(sent[:].rearrange("p (e v d) -> p e v d", e=2, d=D), picked[:], ff_unit[1], half)
+            nc.vector.tensor_reduce(sums[:], sent[:].rearrange("p (v d) -> p v d", d=D), mybir.AxisListType.X, ALU.add)
+            inc[1, half] = sums[:]
+        for t in (2, 3):
+            reflectance(t)
 
-        half = S // 2
-        for h in range(2):
-            hid_bf = keep.tile([P, half, PACK], BF16, name=f"hid_bf{h}", align_bytes=64)
-            hid_codes = keep.tile([P, half], U32, name=f"hid_codes{h}", align_bytes=64)
-            hid_scales = keep.tile([P, half], U8, name=f"hid_scales{h}", align_bytes=64)
-            res = keep.tile([P, half], F32, name=f"res{h}")
-            dst = hid_bf[:].rearrange("p (c i) t -> p c t i", i=4)
-            src = hid_rows[:, :, h * half : (h + 1) * half].rearrange("p t (c i) -> p c t i", i=4)
-            nc.vector.tensor_copy(out=dst, in_=src)
+        reflected = [keep.tile([P, 2, S], F32, name=f"reflected{pair}") for pair in range(2)]
+        for pair, half in parts:
+            reflect(reflected[pair], pair, half, inc[pair, half])
+
+        emi_unit = keep.tile([P, PACK, S], F32, name="emi_unit")
+        inc2 = {}
+        for half in range(2):
+            for pair in range(2):
+                picked = emi_unit[:, 2 * pair + half, :]
+                sent = keep.tile([P, 2 * HALF], F32, name=f"sent_second{pair}{half}")
+                fetch(picked, [reflected[pair][:, 0, :], reflected[pair][:, 1, :]], half)
+                if (pair, half) == (1, 0):
+                    more = keep.tile([P, GROUPS], F32, name="more_plain")
+                    sums = keep.tile([P, GROUPS], F32, name="inc2_plain")
+                    weigh(sent[:].rearrange("p (e v d) -> p e v d", e=2, d=D), picked, ff_sb[pair], half)
+                    nc.vector.tensor_reduce(more[:], sent[:].rearrange("p (v d) -> p v d", d=D), mybir.AxisListType.X, ALU.add)
+                    nc.vector.tensor_tensor(sums[:], more[:], inc[pair, half], ALU.add)
+                    inc2[pair, half] = sums[:]
+                    continue
+                weigh(sent[:].rearrange("p (d e v) -> p e v d", d=D, e=2), picked, ff_sb[pair], half)
+                members = [sent[:, d * GROUPS : (d + 1) * GROUPS] for d in range(D)]
+                bank = bank_of(pair, half)
+                turned = keep.tile([P, GROUPS], F32, name=f"more_turned{pair}{half}")
+                add_turned(bank[:, 0:GROUPS], members if pair == 0 else [inc[pair, half]] + members)
+                if half == 0:
+                    nc.vector.tensor_copy(turned[:], bank[:, 0:GROUPS])
+                else:
+                    nc.scalar.copy(turned[:], bank[:, 0:GROUPS])
+                add_turned(bank[:, GROUPS : 2 * GROUPS], [inc_turned[pair, half], turned[:]] if pair == 0 else [turned[:]])
+                inc2[pair, half] = bank[:, GROUPS : 2 * GROUPS]
+
+        for t in range(PACK):
+            nc.scalar.activation(emi_unit[:, t, :], emi[t][:], ACT.Copy, scale=unit_sb[:, t : t + 1])
+
+        reflected2 = keep.tile([P, PACK, S], F32, name="reflected2")
+
+        def result(piece):
+            c0, c1 = OUT_PIECES[piece]
+            width = c1 - c0
+            hid_bf = keep.tile([P, width, PACK], BF16, name=f"hid_bf{piece}", align_bytes=64)
+            hid_codes = keep.tile([P, width], U32, name=f"hid_codes{piece}", align_bytes=64)
+            hid_scales = keep.tile([P, width], U8, name=f"hid_scales{piece}", align_bytes=64)
+            mixed = keep.tile([P, width], F32, name=f"mixed{piece}")
+            nc.vector.tensor_tensor(
+                hid_bf[:].rearrange("p (c i) t -> p c t i", i=RUN),
+                emi_unit[:, :, c0:c1].rearrange("p t (c i) -> p c t i", i=RUN),
+                reflected2[:, :, c0:c1].rearrange("p t (c i) -> p c t i", i=RUN),
+                ALU.add,
+            )
             nc.vector.quantize_mx(out=hid_codes[:].bitcast(FP8X4), scales=hid_scales[:], in_=hid_bf[:].rearrange("p c t -> p (c t)"))
             nc.tensor.matmul_mx(
-                out=rf[h][:, 0:half], lhsT=w3_codes[:].bitcast(FP8X4), lhsT_scale=w3_scales[:],
-                rhs=hid_codes[:].bitcast(FP8X4), rhs_scale=hid_scales[:], start=True, stop=True,
+                out=rf[piece][:, 0:width],
+                lhsT=w3_codes[:].bitcast(FP8X4),
+                lhsT_scale=w3_scales[:],
+                rhs=hid_codes[:].bitcast(FP8X4),
+                rhs_scale=hid_scales[:],
+                start=True,
+                stop=True,
             )
-            if h == 0:
-                nc.scalar.copy(res[:], rf[h][:, 0:half])
-            else:
-                nc.vector.tensor_copy(res[:], rf[h][:, 0:half])
-            nc.sync.dma_start(out[:, h * half : (h + 1) * half], res[:])
+            nc.scalar.copy(mixed[:], rf[piece][:, 0:width])
+            nc.sync.dma_start(out[:, c0:c1], mixed[:])
+
+        for half in range(2):
+            for pair in range(2):
+                reflect(reflected2[:, 2 * pair : 2 * pair + 2, :], pair, half, inc2[pair, half])
+            for piece, (c0, c1) in enumerate(OUT_PIECES):
+                if c0 // HALF == half:
+                    result(piece)

from contextlib import ExitStack

import concourse.mybir as mybir
from concourse.masks import make_identity

K, T, S, D, N, H = 512, 1024, 512, 4, 128, 512
FLOPS = 2 * K * H * S * 2 + 2 * H * N * S

F32 = mybir.dt.float32
BF16 = mybir.dt.bfloat16
I32 = mybir.dt.int32
U32 = mybir.dt.uint32
U16 = mybir.dt.uint16
U8 = mybir.dt.uint8
FP8X4 = mybir.dt.float8_e4m3fn_x4
ACT = mybir.ActivationFunctionType
ALU = mybir.AluOpType

P = 128
PACK = 4
LIST_ROWS = 16
HALF = S // 2
GROUPS = 2 * HALF // D
RUN = 4
LN_FLOOR = 2.0**-60
OUT_PIECES = ((0, 256), (256, 384), (384, 512))


def tile_picked_yradio_two_p_kernel(tc, x_words, x_scales, w1, w2, ff, unit, w3, offs, see, out):
    nc = tc.nc
    with ExitStack() as ctx:
        keep = ctx.enter_context(tc.tile_pool(name="keep", bufs=1))
        psum = ctx.enter_context(tc.psum_pool(name="psum", bufs=1))

        offs_sb = keep.tile([P, S // LIST_ROWS], U16, name="offs_sb")
        see_sb = keep.tile([P, S // LIST_ROWS], U16, name="see_sb")
        table_scales = keep.tile([P, T], U8, name="table_scales", align_bytes=64)
        table_words = keep.tile([P, T], U32, name="table_words", align_bytes=64)
        w1_raw = keep.tile([P, PACK, H], F32, name="w1_raw")
        w2_raw = keep.tile([P, PACK, H], F32, name="w2_raw")
        w3_raw = keep.tile([P, PACK, N], F32, name="w3_raw")
        unit_sb = keep.tile([P, PACK], F32, name="unit_sb")
        ff_sb = [keep.tile([P, 2, S], F32, name=f"ff_sb{pair}") for pair in range(2)]

        nc.gpsimd.memset(table_scales[:].bitcast(I32), 0)
        nc.sync.dma_start(offs_sb[:], offs)
        for quad in range(4):
            nc.sync.dma_start(
                table_scales[32 * quad : 32 * quad + 4, :].bitcast(I32),
                x_scales[0, 4 * quad : 4 * quad + 4, :].bitcast(I32),
            )
        nc.sync.dma_start(table_words[:].bitcast(I32), x_words[0].rearrange("p c r -> p (c r)").bitcast(I32))
        nc.sync.dma_start(w1_raw[:], w1.rearrange("(p j) c -> p j c", j=PACK))
        nc.sync.dma_start(w2_raw[:], w2.rearrange("(p j) c -> p j c", j=PACK))
        nc.sync.dma_start(see_sb[:], see)
        nc.sync.dma_start(unit_sb[:], unit.rearrange("(p t) o -> p (t o)", t=PACK))
        for pair in range(2):
            nc.sync.dma_start(ff_sb[pair][:], ff.rearrange("(p t) c -> p t c", t=PACK)[:, 2 * pair : 2 * pair + 2, :])
        nc.sync.dma_start(w3_raw[:], w3.rearrange("(p j) c -> p j c", j=PACK))

        ident = keep.tile([P, P], F32, name="ident")
        make_identity(nc, ident[:])
        ln_floor = keep.tile([P, 1], F32, name="ln_floor")
        nc.gpsimd.memset(ln_floor[:], LN_FLOOR)

        x_codes = keep.tile([P, S], U32, name="x_codes", align_bytes=64)
        x_planes = keep.tile([P, S], U8, name="x_planes", align_bytes=64)
        nc.vector.tensor_copy(x_planes[:], table_scales[:].indirect(offs_sb[:]))
        nc.vector.tensor_copy(x_codes[:], table_words[:].indirect(offs_sb[:]))

        def deal_and_round(rounded, raw, t0, t1):
            nc.vector.tensor_copy(
                out=rounded[:, t0:t1, :, :].rearrange("p t m j -> p m j t"),
                in_=raw[:].rearrange("p j (m t) -> p m j t", t=PACK)[:, :, :, t0:t1],
            )

        def quantise(codes, scales, rounded, t0, t1):
            nc.vector.quantize_mx(
                out=codes[:, t0:t1, :].rearrange("p t m -> p (t m)").bitcast(FP8X4),
                scales=scales[:, t0:t1, :].rearrange("p t m -> p (t m)"),
                in_=rounded[:, t0:t1, :, :].rearrange("p t m j -> p (t m j)"),
            )

        def times_patches(bank, codes, scales, t):
            nc.tensor.matmul_mx(
                out=bank[:],
                lhsT=codes[:, t, :].bitcast(FP8X4),
                lhsT_scale=scales[:, t, :],
                rhs=x_codes[:].bitcast(FP8X4),
                rhs_scale=x_planes[:],
                start=True,
                stop=True,
            )

        em = [psum.tile([P, S], F32, name=f"em{t}") for t in range(PACK)]
        rf = [psum.tile([P, S], F32, name=f"rf{t}") for t in range(PACK)]

        w1_bf = keep.tile([P, PACK, P, PACK], BF16, name="w1_bf", align_bytes=64)
        w1_codes = keep.tile([P, PACK, P], U32, name="w1_codes", align_bytes=64)
        w1_scales = keep.tile([P, PACK, P], U8, name="w1_scales", align_bytes=64)
        sig_neg_em = keep.tile([P, PACK, S], F32, name="sig_neg_em")
        for pair in range(2):
            deal_and_round(w1_bf, w1_raw, 2 * pair, 2 * pair + 2)
            for t in (2 * pair, 2 * pair + 1):
                quantise(w1_codes, w1_scales, w1_bf, t, t + 1)
                times_patches(em[t], w1_codes, w1_scales, t)
                nc.scalar.activation(sig_neg_em[:, t, :], em[t][:], ACT.Sigmoid, scale=-1.0)

        w2_bf = keep.tile([P, PACK, P, PACK], BF16, name="w2_bf", align_bytes=64)
        w2_codes = keep.tile([P, PACK, P], U32, name="w2_codes", align_bytes=64)
        w2_scales = keep.tile([P, PACK, P], U8, name="w2_scales", align_bytes=64)
        deal_and_round(w2_bf, w2_raw, 0, PACK)
        quantise(w2_codes, w2_scales, w2_bf, 0, PACK)
        for t in range(PACK):
            times_patches(rf[t], w2_codes, w2_scales, t)

        ff_unit = [keep.tile([P, 2, S], F32, name=f"ff_unit{pair}") for pair in range(2)]
        for t in range(PACK):
            nc.vector.tensor_scalar(ff_unit[t // 2][:, t % 2, :], ff_sb[t // 2][:, t % 2, :], unit_sb[:, t : t + 1], None, ALU.mult)

        w3_bf = keep.tile([P, N, PACK], BF16, name="w3_bf", align_bytes=64)
        w3_codes = keep.tile([P, N], U32, name="w3_codes", align_bytes=64)
        w3_scales = keep.tile([P, N], U8, name="w3_scales", align_bytes=64)
        nc.vector.tensor_copy(
            out=w3_bf[:].rearrange("p (c i) j -> p c j i", i=RUN),
            in_=w3_raw[:].rearrange("p j (c i) -> p c j i", i=RUN),
        )
        nc.vector.quantize_mx(out=w3_codes[:].bitcast(FP8X4), scales=w3_scales[:], in_=w3_bf[:].rearrange("p m j -> p (m j)"))

        log_sig = keep.tile([P, PACK, S], F32, name="log_sig")
        for t in range(PACK):
            nc.scalar.activation(log_sig[:, t, :], sig_neg_em[:, t, :], ACT.Ln, bias=ln_floor[:])

        emi = [keep.tile([P, S], F32, name=f"emi{t}") for t in range(PACK)]
        sig_rf = keep.tile([P, PACK, S], F32, name="sig_rf")

        def emission(t):
            nc.vector.scalar_tensor_tensor(emi[t][:], log_sig[:, t, :], -1.0, em[t][:], ALU.mult, ALU.max)

        def reflectance(t):
            nc.scalar.activation(sig_rf[:, t, :], rf[t][:], ACT.Sigmoid)

        def bank_of(pair, half):
            return em[2 * pair + half]

        def columns(half):
            return slice(half * HALF, (half + 1) * HALF)

        def entries(half):
            return see_sb[:, half * (HALF // LIST_ROWS) : (half + 1) * (HALF // LIST_ROWS)]

        def in_groups(rows):
            return rows.rearrange("p e (v d) -> p e v d", d=D)

        def fetch(picked, windows, half):
            for e in range(2):
                nc.scalar.activation(picked[:, e * HALF : (e + 1) * HALF], windows[e].indirect(entries(half)), ACT.Copy)

        def weigh(sent, picked, factors, half):
            nc.vector.tensor_tensor(sent, picked.rearrange("p (e v d) -> p e v d", e=2, d=D), in_groups(factors[:, :, columns(half)]), ALU.mult)

        def add_turned(target, terms):
            for n, term in enumerate(terms):
                nc.tensor.matmul(target, lhsT=term, rhs=ident[:], is_transpose=True, start=(n == 0), stop=(n == len(terms) - 1))

        def reflect(target, pair, half, sums):
            repeated = sums.rearrange("p (e v) -> p e v", e=2).unsqueeze(3).to_broadcast([P, 2, GROUPS // 2, D])
            nc.vector.scalar_tensor_tensor(
                in_groups(target[:, :, columns(half)]),
                in_groups(sig_rf[:, 2 * pair : 2 * pair + 2, columns(half)]),
                0.9,
                repeated,
                ALU.mult,
                ALU.mult,
            )

        parts = [(pair, half) for pair in range(2) for half in range(2)]
        inc = {}
        inc_turned = {}

        for t in (0, 1):
            reflectance(t)
        for t in (0, 1):
            emission(t)
        for half in range(2):
            sent = keep.tile([P, 2 * HALF], F32, name=f"sent_first0{half}")
            for e in range(2):
                nc.vector.tensor_tensor(
                    sent[:, e * HALF : (e + 1) * HALF], emi[e][:].indirect(entries(half)), ff_unit[0][:, e, columns(half)], ALU.mult
                )
            bank = bank_of(0, half)
            add_turned(bank[:, 0:GROUPS], [sent[:, d : 2 * HALF : D] for d in range(D)])
            turned = keep.tile([P, GROUPS], F32, name=f"inc_turned{half}")
            nc.vector.tensor_copy(turned[:], bank[:, 0:GROUPS])
            add_turned(bank[:, GROUPS : 2 * GROUPS], [turned[:]])
            inc_turned[0, half] = turned[:]
            inc[0, half] = bank[:, GROUPS : 2 * GROUPS]

        for t in (2, 3):
            emission(t)
        for half in range(2):
            picked = keep.tile([P, 2 * HALF], F32, name=f"picked_first{half}")
            sent = keep.tile([P, 2 * HALF], F32, name=f"sent_first1{half}")
            sums = keep.tile([P, GROUPS], F32, name=f"inc_plain{half}")
            fetch(picked, [emi[2][:], emi[3][:]], half)
            weigh(sent[:].rearrange("p (e v d) -> p e v d", e=2, d=D), picked[:], ff_unit[1], half)
            nc.vector.tensor_reduce(sums[:], sent[:].rearrange("p (v d) -> p v d", d=D), mybir.AxisListType.X, ALU.add)
            inc[1, half] = sums[:]
        for t in (2, 3):
            reflectance(t)

        reflected = [keep.tile([P, 2, S], F32, name=f"reflected{pair}") for pair in range(2)]
        for pair, half in parts:
            reflect(reflected[pair], pair, half, inc[pair, half])

        emi_unit = keep.tile([P, PACK, S], F32, name="emi_unit")
        inc2 = {}
        for half in range(2):
            for pair in range(2):
                picked = emi_unit[:, 2 * pair + half, :]
                sent = keep.tile([P, 2 * HALF], F32, name=f"sent_second{pair}{half}")
                fetch(picked, [reflected[pair][:, 0, :], reflected[pair][:, 1, :]], half)
                if (pair, half) == (1, 0):
                    more = keep.tile([P, GROUPS], F32, name="more_plain")
                    sums = keep.tile([P, GROUPS], F32, name="inc2_plain")
                    weigh(sent[:].rearrange("p (e v d) -> p e v d", e=2, d=D), picked, ff_sb[pair], half)
                    nc.vector.tensor_reduce(more[:], sent[:].rearrange("p (v d) -> p v d", d=D), mybir.AxisListType.X, ALU.add)
                    nc.vector.tensor_tensor(sums[:], more[:], inc[pair, half], ALU.add)
                    inc2[pair, half] = sums[:]
                    continue
                weigh(sent[:].rearrange("p (d e v) -> p e v d", d=D, e=2), picked, ff_sb[pair], half)
                members = [sent[:, d * GROUPS : (d + 1) * GROUPS] for d in range(D)]
                bank = bank_of(pair, half)
                turned = keep.tile([P, GROUPS], F32, name=f"more_turned{pair}{half}")
                add_turned(bank[:, 0:GROUPS], members if pair == 0 else [inc[pair, half]] + members)
                if half == 0:
                    nc.vector.tensor_copy(turned[:], bank[:, 0:GROUPS])
                else:
                    nc.scalar.copy(turned[:], bank[:, 0:GROUPS])
                add_turned(bank[:, GROUPS : 2 * GROUPS], [inc_turned[pair, half], turned[:]] if pair == 0 else [turned[:]])
                inc2[pair, half] = bank[:, GROUPS : 2 * GROUPS]

        for t in range(PACK):
            nc.scalar.activation(emi_unit[:, t, :], emi[t][:], ACT.Copy, scale=unit_sb[:, t : t + 1])

        reflected2 = keep.tile([P, PACK, S], F32, name="reflected2")

        def result(piece):
            c0, c1 = OUT_PIECES[piece]
            width = c1 - c0
            hid_bf = keep.tile([P, width, PACK], BF16, name=f"hid_bf{piece}", align_bytes=64)
            hid_codes = keep.tile([P, width], U32, name=f"hid_codes{piece}", align_bytes=64)
            hid_scales = keep.tile([P, width], U8, name=f"hid_scales{piece}", align_bytes=64)
            mixed = keep.tile([P, width], F32, name=f"mixed{piece}")
            nc.vector.tensor_tensor(
                hid_bf[:].rearrange("p (c i) t -> p c t i", i=RUN),
                emi_unit[:, :, c0:c1].rearrange("p t (c i) -> p c t i", i=RUN),
                reflected2[:, :, c0:c1].rearrange("p t (c i) -> p c t i", i=RUN),
                ALU.add,
            )
            nc.vector.quantize_mx(out=hid_codes[:].bitcast(FP8X4), scales=hid_scales[:], in_=hid_bf[:].rearrange("p c t -> p (c t)"))
            nc.tensor.matmul_mx(
                out=rf[piece][:, 0:width],
                lhsT=w3_codes[:].bitcast(FP8X4),
                lhsT_scale=w3_scales[:],
                rhs=hid_codes[:].bitcast(FP8X4),
                rhs_scale=hid_scales[:],
                start=True,
                stop=True,
            )
            nc.scalar.copy(mixed[:], rf[piece][:, 0:width])
            nc.sync.dma_start(out[:, c0:c1], mixed[:])

        for half in range(2):
            for pair in range(2):
                reflect(reflected2[:, 2 * pair : 2 * pair + 2, :], pair, half, inc2[pair, half])
            for piece, (c0, c1) in enumerate(OUT_PIECES):
                if c0 // HALF == half:
                    result(piece)
